import numpy as np
import ml_dtypes


def mxq(x, axis, fmt="e4m3"):
    dtype, down = {"e4m3": (ml_dtypes.float8_e4m3fn, 7), "e5m2": (ml_dtypes.float8_e5m2, 14)}[fmt]
    v = np.moveaxis(np.asarray(x, np.float32).astype(ml_dtypes.bfloat16).astype(np.float64), axis, -1)
    blocks = v.reshape(v.shape[:-1] + (-1, 32))
    amax = np.abs(blocks).max(-1, keepdims=True)
    byte = np.maximum(np.where(amax > 0, np.frexp(amax)[1] - 1 + 127, 0) - down, 1)
    scale = np.exp2(byte - 127.0)
    codes = (blocks / scale).astype(np.float32).astype(dtype).astype(np.float64)
    return np.moveaxis((codes * scale).reshape(v.shape), -1, axis)


WIDE = False


def mx_kscale(k):
    if not WIDE:
        return np.ones(k)
    levels = np.array([10, -10, 5, -5, 0])
    if k % 512:
        return np.exp2(np.random.permutation(np.resize(levels, k // 32))).repeat(32)
    a = np.empty((k // 512, 16))
    for p in range(k // 512):
        a[p, :8] = np.random.permutation(np.resize(levels, 8))
        for g in range(8):
            far = levels[np.abs(levels - a[p, g]) >= 10]
            a[p, g + 8] = far[np.random.randint(len(far))]
    return np.exp2(a.ravel()).repeat(32)


def f64(x):
    return np.asarray(x).astype(np.float64)


def striped(idx):
    return np.tile(idx.reshape(-1, 16).T, (8, 1)).astype(np.uint16)


def unstriped(offs):
    return offs[:16].T.reshape(-1).astype(np.int64)


def striped8(idx):
    return np.concatenate([x.reshape(-1, 16).T for x in idx]).astype(np.uint16)


def runs(offs, k):
    lists = np.stack([offs[16 * r : 16 * r + 16].T.reshape(-1) for r in range(8)]).astype(np.int64)
    return lists[np.arange(k) % 512 // 64]


def pack_weight(w):
    k, n = w.shape
    w = f64(np.asarray(w, np.float32).astype(ml_dtypes.bfloat16)).reshape(k // 32, 32, n)
    amax = np.abs(w).max(1)
    byte = np.clip(np.where(amax > 0, np.frexp(amax)[1] - 1 + 127 - 7, 1), 1, 254)
    scaled = (w * np.exp2(127.0 - byte)[:, None, :]).reshape(k, n).astype(np.float32)
    words = np.ascontiguousarray(scaled.reshape(k // 512, 128, 4, n).transpose(0, 1, 3, 2)).astype(ml_dtypes.float8_e4m3fn).view(np.uint8)
    return words, np.ascontiguousarray(byte.astype(np.uint8).reshape(k // 512, 16, n))


def unpack_weight(words, scales):
    g, p, n, _ = words.shape
    vals = np.ascontiguousarray(words).view(ml_dtypes.float8_e4m3fn).astype(np.float64) * np.repeat(np.exp2(scales.astype(np.float64) - 127.0), 8, axis=1)[..., None]
    return vals.transpose(0, 1, 3, 2).reshape(g * 512, n)


def sigmoid(v):
    return 1.0 / (1.0 + np.exp(-np.maximum(v, -700.0)))

def planes(y):
    n, m = y.shape
    v = y.astype(np.float32).astype(ml_dtypes.bfloat16).astype(np.float64).reshape(n // 32, 32, m)
    top = np.abs(v).max(1)
    byte = np.clip(np.where(top > 0, np.frexp(top)[1] - 1 + 127 - 7, 1), 1, 254)
    codes = (v * np.exp2(127.0 - byte)[:, None, :]).reshape(n, m).astype(np.float32).astype(ml_dtypes.float8_e4m3fn).view(np.uint8)
    words = codes.reshape(n // 512, 128, 4, m).transpose(0, 1, 3, 2)
    return np.ascontiguousarray(words), np.ascontiguousarray(byte.astype(np.uint8).reshape(n // 512, 16, m))


K, T, S, H, W = 512, 2048, 512, 512, 256


def setup_inputs():
    n = np.random.standard_normal
    s = mx_kscale(K)[:, None]
    u = mx_kscale(H)
    packed_xT = pack_weight(n((K, T)) * s)
    packed_w1 = pack_weight(n((K, H)) / np.sqrt(K) / s)
    packed_w2 = pack_weight(n((H, H)) / np.sqrt(H) / u[:, None])
    perm = np.stack([np.random.permutation(S) for _ in range(8)])
    return {
        "x_words": packed_xT[0],
        "x_scales": packed_xT[1],
        "w1_words": packed_w1[0],
        "w1_scales": packed_w1[1],
        "gn": (np.random.uniform(0.5, 1.5, (H, 1)) * u[:, None]).astype(np.float32),
        "w2_words": packed_w2[0],
        "w2_scales": packed_w2[1],
        "offs": striped(np.random.permutation(T)[:S]),
        "n1": striped8(np.stack([np.random.permutation(S) for _ in range(8)])),
        "n2": striped8(np.stack([np.random.permutation(S) for _ in range(8)])),
        "n3": striped8(np.stack([np.random.permutation(S) for _ in range(8)])),
        "n4": striped8(perm[:, :W]),
        "n5": striped8(perm[:, W:]),
        "n6": striped8(np.stack([np.random.permutation(S)[:W] for _ in range(8)])),
        "n7": striped8(np.stack([np.random.permutation(S)[:W] for _ in range(8)])),
    }


def reference(x_words, x_scales, w1_words, w1_scales, gn, w2_words, w2_scales, offs, n1, n2, n3, n4, n5, n6, n7):
    xq = unpack_weight(x_words, x_scales)[:, unstriped(offs)]
    y = unpack_weight(w1_words, w1_scales).T @ xq
    pb = y[np.arange(H)[:, None], runs(n5, H)]
    pa = y[np.arange(H)[:, None], runs(n4, H)]
    rb = pb - (0.5 * pa)
    ra = np.sqrt((pa) ** 2 + (pb) ** 2 + 0.25)
    ds = np.zeros((H, S))
    ds[np.arange(H)[:, None], runs(n4, H)] = ra
    dt = ds.copy()
    dt[np.arange(H)[:, None], runs(n5, H)] = rb
    z2 = f64(gn) * dt
    w2q = unpack_weight(w2_words, w2_scales)
    b = w2q.T @ mxq(z2, 0, "e4m3")
    z = f64(gn) * ((y[np.arange(H)[:, None], runs(n1, H)]) * sigmoid(y) + (y[np.arange(H)[:, None], runs(n2, H)]) * (sigmoid(y[np.arange(H)[:, None], runs(n3, H)])))
    a = w2q.T @ mxq(z, 0, "e4m3")
    ra2 = b[np.arange(H)[:, None], runs(n7, H)] - (0.5 * (a[np.arange(H)[:, None], runs(n6, H)]))
    out = a.copy()
    out[np.arange(H)[:, None], runs(n6, H)] = ra2
    return (out,) + planes(out)

@@ -1,0 +1,244 @@
+from contextlib import ExitStack
+
+import concourse.mybir as mybir
+from concourse.masks import make_identity
+
+F32 = mybir.dt.float32
+BF16 = mybir.dt.bfloat16
+I32 = mybir.dt.int32
+U32 = mybir.dt.uint32
+U16 = mybir.dt.uint16
+U8 = mybir.dt.uint8
+FP8X4 = mybir.dt.float8_e4m3fn_x4
+ACT = mybir.ActivationFunctionType
+MULT = mybir.AluOpType.mult
+ADD = mybir.AluOpType.add
+
+P = 128
+PACK = 4
+T = 2048
+S = 512
+W = 256
+FLOPS = 3 * 2 * 512 * 512 * 512
+
+
+def tile_picked_tieputbwsumpolar_none_po_kernel(
+    tc, x_words, x_scales, w1_words, w1_scales, gn, w2_words, w2_scales,
+    offs, n1, n2, n3, n4, n5, n6, n7, out_0, out_1, out_2,
+):
+    nc = tc.nc
+    with ExitStack() as ctx:
+        lists = ctx.enter_context(tc.tile_pool(name="lists", bufs=1))
+        sb = ctx.enter_context(tc.tile_pool(name="sb", bufs=1))
+        ov = ctx.enter_context(tc.tile_pool(name="ov", bufs=1))
+        ps = ctx.enter_context(tc.psum_pool(name="ps", bufs=1))
+
+        def tile(shape, dtype, name, tag=None):
+            return sb.tile(shape, dtype, name=name, tag=tag or name, align_bytes=64)
+
+        def placed(shape, dtype, name, offset):
+            return ov.tile(shape, dtype, name=name, align_bytes=64, offset=offset)
+
+        def load_list(src, name):
+            dst = lists.tile(list(src.shape), U16, name=name)
+            nc.sync.dma_start(dst[:], src)
+            return dst
+
+        def load_words(src, name):
+            dst = tile([P, src.shape[2]], U32, name)
+            nc.sync.dma_start(dst[:].bitcast(I32), src[0].rearrange("p c r -> p (c r)").bitcast(I32))
+            return dst
+
+        def load_scales(dst, src):
+            for q in range(4):
+                rows = src[0, 4 * q : 4 * q + 4, :].bitcast(I32)
+                nc.sync.dma_start(dst[32 * q : 32 * q + 32, :].bitcast(I32), rows.unsqueeze(0).broadcast_to([8, 4, rows.shape[1]]))
+
+        def deal(words, scales, name):
+            dw = tile([P, S], U32, name + "_dw")
+            ds = tile([P, S], U8, name + "_ds")
+            nc.vector.tensor_copy(
+                dw[:].bitcast(I32).rearrange("p (t m) -> p t m", t=PACK),
+                words[:].bitcast(I32).rearrange("p (m t) -> p t m", t=PACK),
+            )
+            nc.vector.tensor_copy(
+                ds[:].rearrange("p (t m) -> p t m", t=PACK),
+                scales[:].rearrange("p (m t) -> p t m", t=PACK),
+            )
+            return dw, ds
+
+        def product(bank, weights, t, codes, scales, cols):
+            m = slice(t * P, (t + 1) * P)
+            nc.tensor.matmul_mx(
+                out=bank[:, cols],
+                lhsT=weights[0][:, m].bitcast(FP8X4),
+                lhsT_scale=weights[1][:, m],
+                rhs=codes[:, cols].bitcast(FP8X4),
+                rhs_scale=scales[:, cols],
+                start=True,
+                stop=True,
+            )
+
+        def quantize(codes, scales, grouped, cols):
+            nc.vector.quantize_mx(
+                out=codes[:, cols].bitcast(FP8X4),
+                scales=scales[:, cols],
+                in_=grouped.rearrange("p j t -> p (j t)"),
+            )
+
+        halves = [slice(0, W), slice(W, S)]
+        everything = slice(0, S)
+
+        x_sc = tile([P, T], U8, "x_sc")
+        w1_sc = tile([P, S], U8, "w1_sc")
+        w2_sc = tile([P, S], U8, "w2_sc")
+        l_offs = load_list(offs, "l_offs")
+        load_scales(x_sc, x_scales)
+        x_w = load_words(x_words, "x_w")
+        w1_w = load_words(w1_words, "w1_w")
+        load_scales(w1_sc, w1_scales)
+        l4 = load_list(n4, "l4")
+        l5 = load_list(n5, "l5")
+        gain = tile([P, PACK], F32, "gain")
+        nc.sync.dma_start(gain[:], gn.rearrange("(p t) o -> p (t o)", t=PACK))
+        l1 = load_list(n1, "l1")
+        l3 = load_list(n3, "l3")
+        l2 = load_list(n2, "l2")
+        w2_w = load_words(w2_words, "w2_w")
+        load_scales(w2_sc, w2_scales)
+        l6 = load_list(n6, "l6")
+        l7 = load_list(n7, "l7")
+
+        ident = tile([P, P], F32, "ident")
+        make_identity(nc, ident[:])
+        warm = tile([P, 1], F32, "warm")
+        nc.scalar.activation(warm[:], ident[:, 0:1], ACT.Sigmoid)
+
+        xg_s = tile([P, S], U8, "xg_s")
+        xg_w = tile([P, S], U32, "xg_w")
+        nc.vector.tensor_copy(xg_s[:], x_sc[:].indirect(l_offs[:]))
+        w1 = deal(w1_w, w1_sc, "w1")
+        nc.vector.tensor_copy(xg_w[:], x_w[:].indirect(l_offs[:]))
+        w2 = deal(w2_w, w2_sc, "w2")
+
+        y_banks = []
+        for t in range(PACK):
+            bank = ps.tile([P, S], F32, name=f"y_bank{t}", tag=f"A{t}")
+            product(bank, w1, t, xg_w, xg_s, everything)
+            y_banks.append(bank)
+
+        zt_banks = [ps.tile([P, PACK, P], F32, name=f"zt_bank{c}", tag=f"B{c}") for c in range(4)]
+        squares = tile([P, PACK, S], F32, "squares")
+        pairs = []
+        for t in range(PACK):
+            y = tile([P, S], F32, f"y{t}")
+            gy = tile([P, 2 * S], F32, f"gy{t}")
+            sg = tile([P, S], F32, f"sg{t}")
+            s3 = tile([P, S], F32, f"s3_{t}")
+            u1 = tile([P, S], F32, f"u1_{t}")
+            u2 = tile([P, S], F32, f"u2_{t}")
+            nc.scalar.copy(y[:], y_banks[t][:])
+            nc.scalar.activation(gy[:, 0:S], y_banks[t][:], ACT.Copy, scale=gain[:, t : t + 1])
+            nc.scalar.activation(sg[:], y_banks[t][:], ACT.Sigmoid)
+            pair = gy[:, S : 2 * S]
+            nc.vector.tensor_scalar(pair[:, 0:W], y[:].indirect(l4[:]), -0.5, 0.0, MULT, ADD)
+            nc.vector.tensor_copy(pair[:, W:S], y[:].indirect(l5[:]))
+            if t == PACK - 1:
+                nc.scalar.activation(squares[:, t, :], pair, ACT.Square)
+            for h in range(2):
+                nc.scalar.activation(s3[:, halves[h]], y[:].indirect(l3[:, 16 * h : 16 * h + 16]), ACT.Sigmoid)
+            if t < PACK - 1:
+                nc.scalar.activation(squares[:, t, :], pair, ACT.Square)
+            nc.vector.tensor_tensor(u1[:], gy[:].indirect(l1[:]), sg[:], MULT)
+            nc.vector.tensor_tensor(u2[:], gy[:].indirect(l2[:]), s3[:], MULT)
+            for c in range(4):
+                cols = slice(c * P, (c + 1) * P)
+                nc.tensor.matmul(zt_banks[c][:, t, :], u1[:, cols], ident[:], start=True, stop=False, is_transpose=True)
+                nc.tensor.matmul(zt_banks[c][:, t, :], u2[:, cols], ident[:], start=False, stop=True, is_transpose=True)
+            pairs.append(pair)
+
+        sums = tile([P, PACK, W], F32, "sums")
+        nc.vector.scalar_tensor_tensor(sums[:], squares[:, :, 0:W], 4.0, squares[:, :, W:S], MULT, ADD)
+        roots = []
+        for t in range(PACK):
+            root = tile([P, W], F32, f"root{t}")
+            nc.scalar.activation(root[:], sums[:, t, :], ACT.Sqrt, bias=0.25)
+            roots.append(root)
+
+        z_in = tile([P, S, PACK], BF16, "z_in")
+        z_words = z_in[:].rearrange("p j t -> p (j t)").bitcast(F32)
+        for h in range(2):
+            w_bank = ps.tile([P, 2, 2, P], F32, name=f"w_bank{h}", tag=f"A{h}")
+            for b in range(2):
+                c = 2 * h + b
+                zc = placed([P, 2, P, 2], BF16, f"zc{c}", 1536 if c == 3 else 4096 + 1024 * c)
+                nc.scalar.copy(zc[:], zt_banks[c][:].rearrange("j (u e) p -> j u p e", e=2))
+                zc_words = zc[:].rearrange("j u p e -> j (u p e)").bitcast(F32)
+                for u in range(2):
+                    nc.tensor.transpose(w_bank[:, b, u, :], zc_words[:, u * P : (u + 1) * P], ident[:])
+            nc.scalar.copy(
+                z_words[:, h * S : (h + 1) * S].rearrange("p (b j u) -> p b j u", b=2, u=2),
+                w_bank[:].rearrange("p b u j -> p b j u"),
+            )
+        z_w = tile([P, S], U32, "z_w")
+        z_s = tile([P, S], U8, "z_s")
+        quantize(z_w, z_s, z_in[:], everything)
+        outs = []
+        a_banks = []
+        for t in range(PACK):
+            bank = ps.tile([P, S], F32, name=f"a_bank{t}", tag=f"B{t}")
+            product(bank, w2, t, z_w, z_s, everything)
+            a_banks.append(bank)
+
+        z2_in = [placed([P, W, PACK], BF16, f"z2_in{h}", 2048 * h) for h in range(2)]
+        z2_w = tile([P, S], U32, "z2_w")
+        z2_s = tile([P, S], U8, "z2_s")
+        after = ["s3_3", "root0", "z_in", "root2"]
+        for t in range(PACK):
+            dt = tile([P, S], F32, f"dt{t}", tag=after[t])
+            nc.vector.tensor_tensor(dt[:].indirect(l5[:]), pairs[t][:, W:S], pairs[t][:, 0:W], ADD)
+            nc.vector.tensor_copy(dt[:].indirect(l4[:]), roots[t][:])
+            for h in range(2):
+                nc.scalar.activation(z2_in[h][:, :, t], dt[:, halves[h]], ACT.Copy, scale=gain[:, t : t + 1])
+            if t == 1:
+                for k in range(PACK):
+                    o = tile([P, S], F32, f"out{k}")
+                    nc.scalar.copy(o[:], a_banks[k][:])
+                    outs.append(o)
+
+        early = tile([P, 2, W], F32, "early", tag="root3")
+        half_a = [early[:, 0, :], early[:, 1, :]]
+        for t in range(2):
+            nc.vector.tensor_scalar(half_a[t], outs[t][:].indirect(l6[:]), -0.5, 0.0, MULT, ADD)
+        for h in range(2):
+            quantize(z2_w, z2_s, z2_in[h][:], halves[h])
+            late = placed([P, W], F32, f"late{h}", 2048 * h)
+            nc.vector.tensor_scalar(late[:], outs[2 + h][:].indirect(l6[:]), -0.5, 0.0, MULT, ADD)
+            half_a.append(late[:])
+        b_banks = [ps.tile([P, S], F32, name=f"b_bank{t}", tag=f"A{t}") for t in range(PACK)]
+        for t in range(PACK):
+            for cols in halves:
+                product(b_banks[t], w2, t, z2_w, z2_s, cols)
+        bs = []
+        for t in range(PACK):
+            b_sb = tile([P, S], F32, f"b{t}")
+            nc.scalar.copy(b_sb[:], b_banks[t][:])
+            bs.append(b_sb)
+
+        o_in = tile([P, S, PACK], BF16, "o_in")
+        o_w = tile([P, S], U32, "o_w")
+        o_s = tile([P, S], U8, "o_s")
+        out_rows = out_0.rearrange("(p t) j -> p t j", t=PACK)
+        for t in range(PACK):
+            joined = tile([P, W], F32, f"joined{t}")
+            nc.vector.tensor_tensor(joined[:], bs[t][:].indirect(l7[:]), half_a[t], ADD)
+            nc.vector.tensor_copy(outs[t][:].indirect(l6[:]), joined[:])
+            nc.sync.dma_start(out_rows[:, t, :], outs[t][:])
+            for cols in halves if t == PACK - 1 else [everything]:
+                nc.scalar.copy(o_in[:, cols, t], outs[t][:, cols])
+        words_out = out_1[0].rearrange("p c r -> p (c r)").bitcast(I32)
+        for cols in halves:
+            quantize(o_w, o_s, o_in[:, cols, :], cols)
+            nc.sync.dma_start(words_out[:, cols], o_w[:, cols].bitcast(I32))
+        for q in range(4):
+            nc.sync.dma_start(out_2[0, 4 * q : 4 * q + 4, :].bitcast(I32), o_s[32 * q : 32 * q + 4, :].bitcast(I32))

@@ -54,18 +54,11 @@ def tile_picked_tieputbwsumpolar_none_po_kernel(
                 rows = src[0, 4 * q : 4 * q + 4, :].bitcast(I32)
                 nc.sync.dma_start(dst[32 * q : 32 * q + 32, :].bitcast(I32), rows.unsqueeze(0).broadcast_to([8, 4, rows.shape[1]]))
 
-        def deal(words, scales, name):
-            dw = tile([P, S], U32, name + "_dw")
-            ds = tile([P, S], U8, name + "_ds")
+        def deal(dealt, raw, lo, hi):
             nc.vector.tensor_copy(
-                dw[:].bitcast(I32).rearrange("p (t m) -> p t m", t=PACK),
-                words[:].bitcast(I32).rearrange("p (m t) -> p t m", t=PACK),
+                dealt.rearrange("p (t m) -> p m t", t=PACK)[:, :, lo:hi],
+                raw.rearrange("p (m t) -> p m t", t=PACK)[:, :, lo:hi],
             )
-            nc.vector.tensor_copy(
-                ds[:].rearrange("p (t m) -> p t m", t=PACK),
-                scales[:].rearrange("p (m t) -> p t m", t=PACK),
-            )
-            return dw, ds
 
         def product(bank, weights, t, codes, scales, cols):
             m = slice(t * P, (t + 1) * P)
@@ -111,44 +104,67 @@ def tile_picked_tieputbwsumpolar_none_po_kernel(
 
         ident = tile([P, P], F32, "ident")
         make_identity(nc, ident[:])
-        warm = tile([P, 1], F32, "warm")
-        nc.scalar.activation(warm[:], ident[:, 0:1], ACT.Sigmoid)
 
         xg_s = tile([P, S], U8, "xg_s")
         xg_w = tile([P, S], U32, "xg_w")
         nc.vector.tensor_copy(xg_s[:], x_sc[:].indirect(l_offs[:]))
-        w1 = deal(w1_w, w1_sc, "w1")
-        nc.vector.tensor_copy(xg_w[:], x_w[:].indirect(l_offs[:]))
-        w2 = deal(w2_w, w2_sc, "w2")
+        w1 = (tile([P, S], U32, "w1_dw"), tile([P, S], U8, "w1_ds"))
+        w2 = (tile([P, S], U32, "w2_dw"), tile([P, S], U8, "w2_ds"))
+        nc.vector.tensor_copy(xg_w[:, halves[0]], x_w[:].indirect(l_offs[:, 0:16]))
+        deal(w1[0][:].bitcast(I32), w1_w[:].bitcast(I32), 0, 1)
+        deal(w1[1][:], w1_sc[:], 0, 1)
+        nc.vector.tensor_copy(xg_w[:, halves[1]], x_w[:].indirect(l_offs[:, 16:32]))
+        deal(w1[0][:].bitcast(I32), w1_w[:].bitcast(I32), 1, PACK)
+        deal(w1[1][:], w1_sc[:], 1, PACK)
+        deal(w2[0][:].bitcast(I32), w2_w[:].bitcast(I32), 0, PACK)
+        deal(w2[1][:], w2_sc[:], 0, PACK)
 
         y_banks = []
         for t in range(PACK):
             bank = ps.tile([P, S], F32, name=f"y_bank{t}", tag=f"A{t}")
-            product(bank, w1, t, xg_w, xg_s, everything)
-            y_banks.append(bank)
+            if t == 0:
+                other = ps.tile([P, S], F32, name="y_other", tag="B3")
+                y_banks.append([(bank, halves[0]), (other, halves[1])])
+            else:
+                y_banks.append([(bank, everything)])
+            for bank, cols in y_banks[t]:
+                product(bank, w1, t, xg_w, xg_s, cols)
 
         zt_banks = [ps.tile([P, PACK, P], F32, name=f"zt_bank{c}", tag=f"B{c}") for c in range(4)]
-        squares = tile([P, PACK, S], F32, "squares")
         pairs = []
+        sum_banks = []
         for t in range(PACK):
-            y = tile([P, S], F32, f"y{t}")
+            y = placed([P, S], F32, f"y{t}", 8192) if t == 3 else tile([P, S], F32, f"y{t}")
+            sq = placed([P, 4, P], F32, f"sq{t}", 10240) if t == 3 else tile([P, 4, P], F32, f"sq{t}")
             gy = tile([P, 2 * S], F32, f"gy{t}")
             sg = tile([P, S], F32, f"sg{t}")
-            s3 = tile([P, S], F32, f"s3_{t}")
+            s3 = placed([P, S], F32, f"s3_{t}", 13312) if t == 3 else tile([P, S], F32, f"s3_{t}")
             u1 = tile([P, S], F32, f"u1_{t}")
             u2 = tile([P, S], F32, f"u2_{t}")
-            nc.scalar.copy(y[:], y_banks[t][:])
-            nc.scalar.activation(gy[:, 0:S], y_banks[t][:], ACT.Copy, scale=gain[:, t : t + 1])
-            nc.scalar.activation(sg[:], y_banks[t][:], ACT.Sigmoid)
+            if t == 0:
+                bank, cols = y_banks[t][0]
+                nc.scalar.activation(sg[:, cols], bank[:, cols], ACT.Sigmoid)
+            for bank, cols in y_banks[t]:
+                nc.scalar.copy(y[:, cols], bank[:, cols])
+            for bank, cols in y_banks[t]:
+                nc.scalar.activation(gy[:, cols], bank[:, cols], ACT.Copy, scale=gain[:, t : t + 1])
+            for bank, cols in y_banks[t][-1:]:
+                nc.scalar.activation(sg[:, cols], bank[:, cols], ACT.Sigmoid)
             pair = gy[:, S : 2 * S]
             nc.vector.tensor_scalar(pair[:, 0:W], y[:].indirect(l4[:]), -0.5, 0.0, MULT, ADD)
             nc.vector.tensor_copy(pair[:, W:S], y[:].indirect(l5[:]))
-            if t == PACK - 1:
-                nc.scalar.activation(squares[:, t, :], pair, ACT.Square)
+            turned = ps.tile([P, 4, P], F32, name=f"turned{t}", tag=f"A{t}")
+            for c in range(4):
+                nc.tensor.transpose(turned[:, c, :], pair[:, c * P : (c + 1) * P], ident[:])
             for h in range(2):
                 nc.scalar.activation(s3[:, halves[h]], y[:].indirect(l3[:, 16 * h : 16 * h + 16]), ACT.Sigmoid)
-            if t < PACK - 1:
-                nc.scalar.activation(squares[:, t, :], pair, ACT.Square)
+            nc.scalar.activation(sq[:, 0:2, :], turned[:, 0:2, :], ACT.Square, scale=2.0)
+            nc.scalar.activation(sq[:, 2:4, :], turned[:, 2:4, :], ACT.Square)
+            sums = ps.tile([P, 2, P], F32, name=f"sums{t}", tag=f"A{t}")
+            for c in range(2):
+                nc.tensor.matmul(sums[:, c, :], sq[:, c, :], ident[:], start=True, stop=False, is_transpose=True)
+                nc.tensor.matmul(sums[:, c, :], sq[:, 2 + c, :], ident[:], start=False, stop=True, is_transpose=True)
+            sum_banks.append(sums)
             nc.vector.tensor_tensor(u1[:], gy[:].indirect(l1[:]), sg[:], MULT)
             nc.vector.tensor_tensor(u2[:], gy[:].indirect(l2[:]), s3[:], MULT)
             for c in range(4):
@@ -157,15 +173,13 @@ def tile_picked_tieputbwsumpolar_none_po_kernel(
                 nc.tensor.matmul(zt_banks[c][:, t, :], u2[:, cols], ident[:], start=False, stop=True, is_transpose=True)
             pairs.append(pair)
 
-        sums = tile([P, PACK, W], F32, "sums")
-        nc.vector.scalar_tensor_tensor(sums[:], squares[:, :, 0:W], 4.0, squares[:, :, W:S], MULT, ADD)
         roots = []
         for t in range(PACK):
-            root = tile([P, W], F32, f"root{t}")
-            nc.scalar.activation(root[:], sums[:, t, :], ACT.Sqrt, bias=0.25)
+            root = placed([P, W], F32, f"root{t}", 8192 + 1024 * t)
+            nc.scalar.activation(root[:], sum_banks[t][:].rearrange("p c j -> p (c j)"), ACT.Sqrt, bias=0.25)
             roots.append(root)
 
-        z_in = tile([P, S, PACK], BF16, "z_in")
+        z_in = placed([P, S, PACK], BF16, "z_in", 16384)
         z_words = z_in[:].rearrange("p j t -> p (j t)").bitcast(F32)
         for h in range(2):
             w_bank = ps.tile([P, 2, 2, P], F32, name=f"w_bank{h}", tag=f"A{h}")
@@ -193,52 +207,82 @@ def tile_picked_tieputbwsumpolar_none_po_kernel(
         z2_in = [placed([P, W, PACK], BF16, f"z2_in{h}", 2048 * h) for h in range(2)]
         z2_w = tile([P, S], U32, "z2_w")
         z2_s = tile([P, S], U8, "z2_s")
-        after = ["s3_3", "root0", "z_in", "root2"]
-        for t in range(PACK):
-            dt = tile([P, S], F32, f"dt{t}", tag=after[t])
-            nc.vector.tensor_tensor(dt[:].indirect(l5[:]), pairs[t][:, W:S], pairs[t][:, 0:W], ADD)
-            nc.vector.tensor_copy(dt[:].indirect(l4[:]), roots[t][:])
-            for h in range(2):
-                nc.scalar.activation(z2_in[h][:, :, t], dt[:, halves[h]], ACT.Copy, scale=gain[:, t : t + 1])
-            if t == 1:
+        for first in (0, 2):
+            dts = {}
+            for t in (first, first + 1):
+                dts[t] = placed([P, S], F32, f"dt{t}", 12288 + 2048 * t)
+                nc.vector.tensor_tensor(dts[t][:].indirect(l5[:]), pairs[t][:, W:S], pairs[t][:, 0:W], ADD)
+            for t in (first, first + 1):
+                dt = dts[t]
+                nc.vector.tensor_copy(dt[:].indirect(l4[:]), roots[t][:])
+                for h in range(2):
+                    nc.scalar.activation(z2_in[h][:, :, t], dt[:, halves[h]], ACT.Copy, scale=gain[:, t : t + 1])
+            if first == 0:
                 for k in range(PACK):
-                    o = tile([P, S], F32, f"out{k}")
+                    o = tile([P, S], F32, f"a{k}")
                     nc.scalar.copy(o[:], a_banks[k][:])
                     outs.append(o)
 
-        early = tile([P, 2, W], F32, "early", tag="root3")
+        early = placed([P, 2, W], F32, "early", 11264)
         half_a = [early[:, 0, :], early[:, 1, :]]
         for t in range(2):
             nc.vector.tensor_scalar(half_a[t], outs[t][:].indirect(l6[:]), -0.5, 0.0, MULT, ADD)
         for h in range(2):
             quantize(z2_w, z2_s, z2_in[h][:], halves[h])
-            late = placed([P, W], F32, f"late{h}", 2048 * h)
+        for h in range(2):
+            late = placed([P, W], F32, f"late{h}", 2048 + 1024 * h)
             nc.vector.tensor_scalar(late[:], outs[2 + h][:].indirect(l6[:]), -0.5, 0.0, MULT, ADD)
             half_a.append(late[:])
         b_banks = [ps.tile([P, S], F32, name=f"b_bank{t}", tag=f"A{t}") for t in range(PACK)]
         for t in range(PACK):
-            for cols in halves:
+            for cols in halves if t == 0 else [everything]:
                 product(b_banks[t], w2, t, z2_w, z2_s, cols)
-        bs = []
-        for t in range(PACK):
-            b_sb = tile([P, S], F32, f"b{t}")
-            nc.scalar.copy(b_sb[:], b_banks[t][:])
-            bs.append(b_sb)
 
         o_in = tile([P, S, PACK], BF16, "o_in")
         o_w = tile([P, S], U32, "o_w")
         o_s = tile([P, S], U8, "o_s")
         out_rows = out_0.rearrange("(p t) j -> p t j", t=PACK)
-        for t in range(PACK):
-            joined = tile([P, W], F32, f"joined{t}")
-            nc.vector.tensor_tensor(joined[:], bs[t][:].indirect(l7[:]), half_a[t], ADD)
-            nc.vector.tensor_copy(outs[t][:].indirect(l6[:]), joined[:])
-            nc.sync.dma_start(out_rows[:, t, :], outs[t][:])
-            for cols in halves if t == PACK - 1 else [everything]:
-                nc.scalar.copy(o_in[:, cols, t], outs[t][:, cols])
         words_out = out_1[0].rearrange("p c r -> p (c r)").bitcast(I32)
+        joined = []
+
+        def join(t):
+            b_sb = tile([P, S], F32, f"b{t}")
+            nc.scalar.copy(b_sb[:], b_banks[t][:])
+            joined.append(tile([P, W], F32, f"joined{t}"))
+            nc.vector.tensor_tensor(joined[t][:], b_sb[:].indirect(l7[:]), half_a[t], ADD)
+
+        def put(t):
+            res = tile([P, S], F32, f"res{t}", tag=f"b{t}")
+            nc.scalar.copy(res[:], a_banks[t][:])
+            nc.vector.tensor_copy(res[:].indirect(l6[:]), joined[t][:])
+            nc.sync.dma_start(out_rows[:, t, :], res[:])
+            return res
+
+        def regroup(t, res):
+            if t < 2:
+                nc.scalar.copy(o_in[:, :, t], res[:])
+            elif t == 2:
+                nc.scalar.copy(o_in[:, 0:W, 2:4], res[:, 0:W].unsqueeze(2).broadcast_to([P, W, 2]))
+                nc.scalar.copy(o_in[:, W:S, 2], res[:, W:S])
+            else:
+                nc.vector.tensor_copy(o_in[:, 0:W, 3], res[:, 0:W])
+                nc.scalar.copy(o_in[:, W:S, 3], res[:, W:S])
+
+        join(0)
+        join(1)
+        r0 = put(0)
+        join(2)
+        r1 = put(1)
+        join(3)
+        regroup(0, r0)
+        r2 = put(2)
+        regroup(1, r1)
+        r3 = put(3)
+        regroup(2, r2)
+        regroup(3, r3)
         for cols in halves:
             quantize(o_w, o_s, o_in[:, cols, :], cols)
             nc.sync.dma_start(words_out[:, cols], o_w[:, cols].bitcast(I32))
         for q in range(4):
-            nc.sync.dma_start(out_2[0, 4 * q : 4 * q + 4, :].bitcast(I32), o_s[32 * q : 32 * q + 4, :].bitcast(I32))
+            queue = nc.scalar if q % 2 else nc.sync
+            queue.dma_start(out_2[0, 4 * q : 4 * q + 4, :].bitcast(I32), o_s[32 * q : 32 * q + 4, :].bitcast(I32))

@@ -90,15 +90,15 @@ def tile_picked_tieputbwsumpolar_none_po_kernel(
         x_w = load_words(x_words, "x_w")
         w1_w = load_words(w1_words, "w1_w")
         load_scales(w1_sc, w1_scales)
+        w2_w = load_words(w2_words, "w2_w")
         l4 = load_list(n4, "l4")
         l5 = load_list(n5, "l5")
         gain = tile([P, PACK], F32, "gain")
         nc.sync.dma_start(gain[:], gn.rearrange("(p t) o -> p (t o)", t=PACK))
+        load_scales(w2_sc, w2_scales)
         l1 = load_list(n1, "l1")
         l3 = load_list(n3, "l3")
         l2 = load_list(n2, "l2")
-        w2_w = load_words(w2_words, "w2_w")
-        load_scales(w2_sc, w2_scales)
         l6 = load_list(n6, "l6")
         l7 = load_list(n7, "l7")
 

@@ -104,6 +104,8 @@ def tile_picked_tieputbwsumpolar_none_po_kernel(
 
         ident = tile([P, P], F32, "ident")
         make_identity(nc, ident[:])
+        warm = tile([P, 1], F32, "warm")
+        nc.scalar.activation(warm[:], ident[:, 0:1], ACT.Sigmoid)
 
         xg_s = tile([P, S], U8, "xg_s")
         xg_w = tile([P, S], U32, "xg_w")
@@ -141,14 +143,11 @@ def tile_picked_tieputbwsumpolar_none_po_kernel(
             s3 = placed([P, S], F32, f"s3_{t}", 13312) if t == 3 else tile([P, S], F32, f"s3_{t}")
             u1 = tile([P, S], F32, f"u1_{t}")
             u2 = tile([P, S], F32, f"u2_{t}")
-            if t == 0:
-                bank, cols = y_banks[t][0]
-                nc.scalar.activation(sg[:, cols], bank[:, cols], ACT.Sigmoid)
             for bank, cols in y_banks[t]:
                 nc.scalar.copy(y[:, cols], bank[:, cols])
             for bank, cols in y_banks[t]:
                 nc.scalar.activation(gy[:, cols], bank[:, cols], ACT.Copy, scale=gain[:, t : t + 1])
-            for bank, cols in y_banks[t][-1:]:
+            for bank, cols in y_banks[t]:
                 nc.scalar.activation(sg[:, cols], bank[:, cols], ACT.Sigmoid)
             pair = gy[:, S : 2 * S]
             nc.vector.tensor_scalar(pair[:, 0:W], y[:].indirect(l4[:]), -0.5, 0.0, MULT, ADD)

from contextlib import ExitStack

import concourse.mybir as mybir
from concourse.masks import make_identity

F32 = mybir.dt.float32
BF16 = mybir.dt.bfloat16
I32 = mybir.dt.int32
U32 = mybir.dt.uint32
U16 = mybir.dt.uint16
U8 = mybir.dt.uint8
FP8X4 = mybir.dt.float8_e4m3fn_x4
ACT = mybir.ActivationFunctionType
MULT = mybir.AluOpType.mult
ADD = mybir.AluOpType.add

P = 128
PACK = 4
T = 2048
S = 512
W = 256
FLOPS = 3 * 2 * 512 * 512 * 512


def tile_picked_tieputbwsumpolar_none_po_kernel(
    tc, x_words, x_scales, w1_words, w1_scales, gn, w2_words, w2_scales,
    offs, n1, n2, n3, n4, n5, n6, n7, out_0, out_1, out_2,
):
    nc = tc.nc
    with ExitStack() as ctx:
        lists = ctx.enter_context(tc.tile_pool(name="lists", bufs=1))
        sb = ctx.enter_context(tc.tile_pool(name="sb", bufs=1))
        ov = ctx.enter_context(tc.tile_pool(name="ov", bufs=1))
        ps = ctx.enter_context(tc.psum_pool(name="ps", bufs=1))

        def tile(shape, dtype, name, tag=None):
            return sb.tile(shape, dtype, name=name, tag=tag or name, align_bytes=64)

        def placed(shape, dtype, name, offset):
            return ov.tile(shape, dtype, name=name, align_bytes=64, offset=offset)

        def load_list(src, name):
            dst = lists.tile(list(src.shape), U16, name=name)
            nc.sync.dma_start(dst[:], src)
            return dst

        def load_words(src, name):
            dst = tile([P, src.shape[2]], U32, name)
            nc.sync.dma_start(dst[:].bitcast(I32), src[0].rearrange("p c r -> p (c r)").bitcast(I32))
            return dst

        def load_scales(dst, src):
            for q in range(4):
                rows = src[0, 4 * q : 4 * q + 4, :].bitcast(I32)
                nc.sync.dma_start(dst[32 * q : 32 * q + 32, :].bitcast(I32), rows.unsqueeze(0).broadcast_to([8, 4, rows.shape[1]]))

        def deal(dealt, raw, lo, hi):
            nc.vector.tensor_copy(
                dealt.rearrange("p (t m) -> p m t", t=PACK)[:, :, lo:hi],
                raw.rearrange("p (m t) -> p m t", t=PACK)[:, :, lo:hi],
            )

        def product(bank, weights, t, codes, scales, cols):
            m = slice(t * P, (t + 1) * P)
            nc.tensor.matmul_mx(
                out=bank[:, cols],
                lhsT=weights[0][:, m].bitcast(FP8X4),
                lhsT_scale=weights[1][:, m],
                rhs=codes[:, cols].bitcast(FP8X4),
                rhs_scale=scales[:, cols],
                start=True,
                stop=True,
            )

        def quantize(codes, scales, grouped, cols):
            nc.vector.quantize_mx(
                out=codes[:, cols].bitcast(FP8X4),
                scales=scales[:, cols],
                in_=grouped.rearrange("p j t -> p (j t)"),
            )

        halves = [slice(0, W), slice(W, S)]
        everything = slice(0, S)

        x_sc = tile([P, T], U8, "x_sc")
        w1_sc = tile([P, S], U8, "w1_sc")
        w2_sc = tile([P, S], U8, "w2_sc")
        l_offs = load_list(offs, "l_offs")
        load_scales(x_sc, x_scales)
        x_w = load_words(x_words, "x_w")
        w1_w = load_words(w1_words, "w1_w")
        load_scales(w1_sc, w1_scales)
        w2_w = load_words(w2_words, "w2_w")
        l4 = load_list(n4, "l4")
        l5 = load_list(n5, "l5")
        gain = tile([P, PACK], F32, "gain")
        nc.sync.dma_start(gain[:], gn.rearrange("(p t) o -> p (t o)", t=PACK))
        load_scales(w2_sc, w2_scales)
        l1 = load_list(n1, "l1")
        l3 = load_list(n3, "l3")
        l2 = load_list(n2, "l2")
        l6 = load_list(n6, "l6")
        l7 = load_list(n7, "l7")

        ident = tile([P, P], F32, "ident")
        make_identity(nc, ident[:])
        warm = tile([P, 1], F32, "warm")
        nc.scalar.activation(warm[:], ident[:, 0:1], ACT.Sigmoid)

        xg_s = tile([P, S], U8, "xg_s")
        xg_w = tile([P, S], U32, "xg_w")
        nc.vector.tensor_copy(xg_s[:], x_sc[:].indirect(l_offs[:]))
        w1 = (tile([P, S], U32, "w1_dw"), tile([P, S], U8, "w1_ds"))
        w2 = (tile([P, S], U32, "w2_dw"), tile([P, S], U8, "w2_ds"))
        nc.vector.tensor_copy(xg_w[:, halves[0]], x_w[:].indirect(l_offs[:, 0:16]))
        deal(w1[0][:].bitcast(I32), w1_w[:].bitcast(I32), 0, 1)
        deal(w1[1][:], w1_sc[:], 0, 1)
        nc.vector.tensor_copy(xg_w[:, halves[1]], x_w[:].indirect(l_offs[:, 16:32]))
        deal(w1[0][:].bitcast(I32), w1_w[:].bitcast(I32), 1, PACK)
        deal(w1[1][:], w1_sc[:], 1, PACK)
        deal(w2[0][:].bitcast(I32), w2_w[:].bitcast(I32), 0, PACK)
        deal(w2[1][:], w2_sc[:], 0, PACK)

        y_banks = []
        for t in range(PACK):
            bank = ps.tile([P, S], F32, name=f"y_bank{t}", tag=f"A{t}")
            if t == 0:
                other = ps.tile([P, S], F32, name="y_other", tag="B3")
                y_banks.append([(bank, halves[0]), (other, halves[1])])
            else:
                y_banks.append([(bank, everything)])
            for bank, cols in y_banks[t]:
                product(bank, w1, t, xg_w, xg_s, cols)

        zt_banks = [ps.tile([P, PACK, P], F32, name=f"zt_bank{c}", tag=f"B{c}") for c in range(4)]
        pairs = []
        sum_banks = []
        for t in range(PACK):
            y = placed([P, S], F32, f"y{t}", 8192) if t == 3 else tile([P, S], F32, f"y{t}")
            sq = placed([P, 4, P], F32, f"sq{t}", 10240) if t == 3 else tile([P, 4, P], F32, f"sq{t}")
            gy = tile([P, 2 * S], F32, f"gy{t}")
            sg = tile([P, S], F32, f"sg{t}")
            s3 = placed([P, S], F32, f"s3_{t}", 13312) if t == 3 else tile([P, S], F32, f"s3_{t}")
            u1 = tile([P, S], F32, f"u1_{t}")
            u2 = tile([P, S], F32, f"u2_{t}")
            for bank, cols in y_banks[t]:
                nc.scalar.copy(y[:, cols], bank[:, cols])
            for bank, cols in y_banks[t]:
                nc.scalar.activation(gy[:, cols], bank[:, cols], ACT.Copy, scale=gain[:, t : t + 1])
            for bank, cols in y_banks[t]:
                nc.scalar.activation(sg[:, cols], bank[:, cols], ACT.Sigmoid)
            pair = gy[:, S : 2 * S]
            nc.vector.tensor_scalar(pair[:, 0:W], y[:].indirect(l4[:]), -0.5, 0.0, MULT, ADD)
            nc.vector.tensor_copy(pair[:, W:S], y[:].indirect(l5[:]))
            turned = ps.tile([P, 4, P], F32, name=f"turned{t}", tag=f"A{t}")
            for c in range(4):
                nc.tensor.transpose(turned[:, c, :], pair[:, c * P : (c + 1) * P], ident[:])
            for h in range(2):
                nc.scalar.activation(s3[:, halves[h]], y[:].indirect(l3[:, 16 * h : 16 * h + 16]), ACT.Sigmoid)
            nc.scalar.activation(sq[:, 0:2, :], turned[:, 0:2, :], ACT.Square, scale=2.0)
            nc.scalar.activation(sq[:, 2:4, :], turned[:, 2:4, :], ACT.Square)
            sums = ps.tile([P, 2, P], F32, name=f"sums{t}", tag=f"A{t}")
            for c in range(2):
                nc.tensor.matmul(sums[:, c, :], sq[:, c, :], ident[:], start=True, stop=False, is_transpose=True)
                nc.tensor.matmul(sums[:, c, :], sq[:, 2 + c, :], ident[:], start=False, stop=True, is_transpose=True)
            sum_banks.append(sums)
            nc.vector.tensor_tensor(u1[:], gy[:].indirect(l1[:]), sg[:], MULT)
            nc.vector.tensor_tensor(u2[:], gy[:].indirect(l2[:]), s3[:], MULT)
            for c in range(4):
                cols = slice(c * P, (c + 1) * P)
                nc.tensor.matmul(zt_banks[c][:, t, :], u1[:, cols], ident[:], start=True, stop=False, is_transpose=True)
                nc.tensor.matmul(zt_banks[c][:, t, :], u2[:, cols], ident[:], start=False, stop=True, is_transpose=True)
            pairs.append(pair)

        roots = []
        for t in range(PACK):
            root = placed([P, W], F32, f"root{t}", 8192 + 1024 * t)
            nc.scalar.activation(root[:], sum_banks[t][:].rearrange("p c j -> p (c j)"), ACT.Sqrt, bias=0.25)
            roots.append(root)

        z_in = placed([P, S, PACK], BF16, "z_in", 16384)
        z_words = z_in[:].rearrange("p j t -> p (j t)").bitcast(F32)
        for h in range(2):
            w_bank = ps.tile([P, 2, 2, P], F32, name=f"w_bank{h}", tag=f"A{h}")
            for b in range(2):
                c = 2 * h + b
                zc = placed([P, 2, P, 2], BF16, f"zc{c}", 1536 if c == 3 else 4096 + 1024 * c)
                nc.scalar.copy(zc[:], zt_banks[c][:].rearrange("j (u e) p -> j u p e", e=2))
                zc_words = zc[:].rearrange("j u p e -> j (u p e)").bitcast(F32)
                for u in range(2):
                    nc.tensor.transpose(w_bank[:, b, u, :], zc_words[:, u * P : (u + 1) * P], ident[:])
            nc.scalar.copy(
                z_words[:, h * S : (h + 1) * S].rearrange("p (b j u) -> p b j u", b=2, u=2),
                w_bank[:].rearrange("p b u j -> p b j u"),
            )
        z_w = tile([P, S], U32, "z_w")
        z_s = tile([P, S], U8, "z_s")
        quantize(z_w, z_s, z_in[:], everything)
        outs = []
        a_banks = []
        for t in range(PACK):
            bank = ps.tile([P, S], F32, name=f"a_bank{t}", tag=f"B{t}")
            product(bank, w2, t, z_w, z_s, everything)
            a_banks.append(bank)

        z2_in = [placed([P, W, PACK], BF16, f"z2_in{h}", 2048 * h) for h in range(2)]
        z2_w = tile([P, S], U32, "z2_w")
        z2_s = tile([P, S], U8, "z2_s")
        for first in (0, 2):
            dts = {}
            for t in (first, first + 1):
                dts[t] = placed([P, S], F32, f"dt{t}", 12288 + 2048 * t)
                nc.vector.tensor_tensor(dts[t][:].indirect(l5[:]), pairs[t][:, W:S], pairs[t][:, 0:W], ADD)
            for t in (first, first + 1):
                dt = dts[t]
                nc.vector.tensor_copy(dt[:].indirect(l4[:]), roots[t][:])
                for h in range(2):
                    nc.scalar.activation(z2_in[h][:, :, t], dt[:, halves[h]], ACT.Copy, scale=gain[:, t : t + 1])
            if first == 0:
                for k in range(PACK):
                    o = tile([P, S], F32, f"a{k}")
                    nc.scalar.copy(o[:], a_banks[k][:])
                    outs.append(o)

        early = placed([P, 2, W], F32, "early", 11264)
        half_a = [early[:, 0, :], early[:, 1, :]]
        for t in range(2):
            nc.vector.tensor_scalar(half_a[t], outs[t][:].indirect(l6[:]), -0.5, 0.0, MULT, ADD)
        for h in range(2):
            quantize(z2_w, z2_s, z2_in[h][:], halves[h])
        for h in range(2):
            late = placed([P, W], F32, f"late{h}", 2048 + 1024 * h)
            nc.vector.tensor_scalar(late[:], outs[2 + h][:].indirect(l6[:]), -0.5, 0.0, MULT, ADD)
            half_a.append(late[:])
        b_banks = [ps.tile([P, S], F32, name=f"b_bank{t}", tag=f"A{t}") for t in range(PACK)]
        for t in range(PACK):
            for cols in halves if t == 0 else [everything]:
                product(b_banks[t], w2, t, z2_w, z2_s, cols)

        o_in = tile([P, S, PACK], BF16, "o_in")
        o_w = tile([P, S], U32, "o_w")
        o_s = tile([P, S], U8, "o_s")
        out_rows = out_0.rearrange("(p t) j -> p t j", t=PACK)
        words_out = out_1[0].rearrange("p c r -> p (c r)").bitcast(I32)
        joined = []

        def join(t):
            b_sb = tile([P, S], F32, f"b{t}")
            nc.scalar.copy(b_sb[:], b_banks[t][:])
            joined.append(tile([P, W], F32, f"joined{t}"))
            nc.vector.tensor_tensor(joined[t][:], b_sb[:].indirect(l7[:]), half_a[t], ADD)

        def put(t):
            res = tile([P, S], F32, f"res{t}", tag=f"b{t}")
            nc.scalar.copy(res[:], a_banks[t][:])
            nc.vector.tensor_copy(res[:].indirect(l6[:]), joined[t][:])
            nc.sync.dma_start(out_rows[:, t, :], res[:])
            return res

        def regroup(t, res):
            if t < 2:
                nc.scalar.copy(o_in[:, :, t], res[:])
            elif t == 2:
                nc.scalar.copy(o_in[:, 0:W, 2:4], res[:, 0:W].unsqueeze(2).broadcast_to([P, W, 2]))
                nc.scalar.copy(o_in[:, W:S, 2], res[:, W:S])
            else:
                nc.vector.tensor_copy(o_in[:, 0:W, 3], res[:, 0:W])
                nc.scalar.copy(o_in[:, W:S, 3], res[:, W:S])

        join(0)
        join(1)
        r0 = put(0)
        join(2)
        r1 = put(1)
        join(3)
        regroup(0, r0)
        r2 = put(2)
        regroup(1, r1)
        r3 = put(3)
        regroup(2, r2)
        regroup(3, r3)
        for cols in halves:
            quantize(o_w, o_s, o_in[:, cols, :], cols)
            nc.sync.dma_start(words_out[:, cols], o_w[:, cols].bitcast(I32))
        for q in range(4):
            queue = nc.scalar if q % 2 else nc.sync
            queue.dma_start(out_2[0, 4 * q : 4 * q + 4, :].bitcast(I32), o_s[32 * q : 32 * q + 4, :].bitcast(I32))
